import numpy as np
import ml_dtypes


def mxq(x, axis, fmt="e4m3"):
    dtype, down = {"e4m3": (ml_dtypes.float8_e4m3fn, 7), "e5m2": (ml_dtypes.float8_e5m2, 14)}[fmt]
    v = np.moveaxis(np.asarray(x, np.float32).astype(ml_dtypes.bfloat16).astype(np.float64), axis, -1)
    blocks = v.reshape(v.shape[:-1] + (-1, 32))
    amax = np.abs(blocks).max(-1, keepdims=True)
    byte = np.maximum(np.where(amax > 0, np.frexp(amax)[1] - 1 + 127, 0) - down, 1)
    scale = np.exp2(byte - 127.0)
    codes = (blocks / scale).astype(np.float32).astype(dtype).astype(np.float64)
    return np.moveaxis((codes * scale).reshape(v.shape), -1, axis)


WIDE = False


def mx_kscale(k):
    if not WIDE:
        return np.ones(k)
    levels = np.array([10, -10, 5, -5, 0])
    if k % 512:
        return np.exp2(np.random.permutation(np.resize(levels, k // 32))).repeat(32)
    a = np.empty((k // 512, 16))
    for p in range(k // 512):
        a[p, :8] = np.random.permutation(np.resize(levels, 8))
        for g in range(8):
            far = levels[np.abs(levels - a[p, g]) >= 10]
            a[p, g + 8] = far[np.random.randint(len(far))]
    return np.exp2(a.ravel()).repeat(32)


def f64(x):
    return np.asarray(x).astype(np.float64)


def striped(idx):
    return np.tile(np.asarray(idx).reshape(-1, 16).T, (8, 1)).astype(np.uint16)


def unstriped(offs):
    return offs[:16].T.reshape(-1).astype(np.int64)


E2M1 = np.array([0.0, 0.5, 1.0, 1.5, 2.0, 3.0, 4.0, 6.0, -0.0, -0.5, -1.0, -1.5, -2.0, -3.0, -4.0, -6.0])


def pack_weight(w, fmt):
    k, n = w.shape
    w = f64(np.asarray(w, np.float32).astype(ml_dtypes.bfloat16)).reshape(k // 32, 32, n)
    amax = np.abs(w).max(1)
    if fmt == "e4m3":
        byte = np.frexp(amax)[1] - 1 + 127 - 7
    else:
        mant, ex = np.frexp(amax / 6.0)
        byte = np.where(mant > 0.5, ex, ex - 1) + 127
    byte = np.clip(np.where(amax > 0, byte, 1), 1, 254)
    scaled = (w * np.exp2(127.0 - byte)[:, None, :]).reshape(k, n).astype(np.float32)
    by_word = np.ascontiguousarray(scaled.reshape(k // 512, 128, 4, n).transpose(0, 1, 3, 2))
    if fmt == "e4m3":
        words = by_word.astype(ml_dtypes.float8_e4m3fn).view(np.uint8)
    else:
        c = by_word.astype(ml_dtypes.float4_e2m1fn).view(np.uint8) & 0xF
        words = (c[..., 0::2] | (c[..., 1::2] << 4)).reshape(k // 512, 128, 2 * n)
    return np.ascontiguousarray(words), np.ascontiguousarray(byte.astype(np.uint8).reshape(k // 512, 16, n))


def unpack_weight(words, scales, fmt):
    g, _, n = scales.shape
    words = np.ascontiguousarray(words).reshape(g, 128, n, -1)
    if fmt == "e4m3":
        vals = words.view(ml_dtypes.float8_e4m3fn).astype(np.float64)
    else:
        nib = np.empty((g, 128, n, 4), np.uint8)
        nib[..., 0::2] = words & 0xF
        nib[..., 1::2] = words >> 4
        vals = E2M1[nib]
    vals = vals * np.repeat(np.exp2(scales.astype(np.float64) - 127.0), 8, axis=1)[..., None]
    return vals.transpose(0, 1, 3, 2).reshape(g * 512, n)


D, U, T, I, V, Q = 512, 512, 2048, 256, 1024, 256


def setup_inputs():
    n = np.random.standard_normal
    idx = np.random.permutation(T)[:U]
    idx2 = np.random.permutation(U)[:I]
    idx3 = np.random.permutation(V)[:I]
    fd = mx_kscale(D)
    summp = pack_weight(n((D, T)) / fd[:, None], "e4m3")
    return {
        "query": (n((D, Q)) * 0.7 / np.sqrt(D) * fd[:, None]).astype(np.float32),
        "dquery": (n((D, Q)) * 1.0 / np.sqrt(D) * fd[:, None]).astype(np.float32),
        "summ_words": summp[0],
        "summ_scales": summp[1],
        "base": (0.002 * n((Q, V))).astype(np.float32),
        "gain": (np.random.uniform(0.5, 2.0, (1, I))).astype(np.float32),
        "offs": striped(idx),
        "offs2": striped(idx2),
        "offs3": striped(idx3),
    }


def reference(query, dquery, summ_words, summ_scales, base, gain, offs, offs2, offs3):
    idx = unstriped(offs)
    idx2 = unstriped(offs2)
    idx3 = unstriped(offs3)
    summu = unpack_weight(summ_words, summ_scales, "e4m3")
    queryq = mxq(f64(query), 0, "e4m3")
    summidxg = summu[:, idx]
    a = queryq.T @ summidxg
    dqueryq = mxq(f64(dquery), 0, "e4m3")
    b = dqueryq.T @ summidxg
    p = np.exp(a - np.max(a, axis=1, keepdims=True))
    w = p / np.sum(p, axis=1, keepdims=True)
    dw = w * (b - np.sum(w * b, axis=1, keepdims=True))
    y = (dw[:, idx2] * f64(gain) + f64(base)[:, idx3]) * 512.0
    return y

@@ -1,0 +1,136 @@
+from contextlib import ExitStack
+
+import concourse.mybir as mybir
+
+D, U, T, I, V, Q = 512, 512, 2048, 256, 1024, 256
+FLOPS = 2 * 2 * D * Q * U
+
+F32 = mybir.dt.float32
+BF16 = mybir.dt.bfloat16
+I32 = mybir.dt.int32
+U32 = mybir.dt.uint32
+U16 = mybir.dt.uint16
+U8 = mybir.dt.uint8
+FP8X4 = mybir.dt.float8_e4m3fn_x4
+ALU = mybir.AluOpType
+ACT = mybir.ActivationFunctionType
+AXIS = mybir.AxisListType
+
+P = 128
+PACK = 4
+TILES = Q // P
+OUT_SCALE = 512.0
+
+
+def tile_attend_masstangent_kernel(tc, query, dquery, summ_words, summ_scales, base, gain, offs, offs2, offs3, out):
+    nc = tc.nc
+    with ExitStack() as ctx:
+        sb = ctx.enter_context(tc.tile_pool(name="sb", bufs=1))
+        late = ctx.enter_context(tc.tile_pool(name="late", bufs=1))
+        ps = ctx.enter_context(tc.psum_pool(name="ps", bufs=1))
+
+        page_list = sb.tile([P, U // 16], U16, name="page_list")
+        mass_list = sb.tile([P, I // 16], U16, name="mass_list")
+        base_list = sb.tile([P, I // 16], U16, name="base_list")
+        store_scales = sb.tile([P, T], U8, name="store_scales", align_bytes=64)
+        gain_pairs = sb.tile([P, 2], F32, name="gain_pairs")
+
+        nc.gpsimd.memset(store_scales[:].bitcast(I32), 0)
+        nc.sync.dma_start(page_list[:], offs)
+        nc.sync.dma_start(base_list[:], offs3)
+        nc.sync.dma_start(mass_list[:], offs2)
+        for quad in range(4):
+            nc.sync.dma_start(
+                store_scales[32 * quad : 32 * quad + 4, :].bitcast(I32),
+                summ_scales[0, 4 * quad : 4 * quad + 4, :].bitcast(I32),
+            )
+
+        zeros = late.tile([P, 4 * V + T], F32, name="zeros", offset=0)
+        ident = sb.tile([P, P], F32, name="ident")
+        nc.gpsimd.memset(zeros[:, :P], 0.0)
+        nc.gpsimd.affine_select(
+            out=ident[:], in_=zeros[:, :P], compare_op=ALU.not_equal, fill=1.0, base=0, pattern=[[-1, P]], channel_multiplier=1
+        )
+        nc.gpsimd.dma_start(gain_pairs[:], gain.rearrange("o (p c) -> (o p) c", c=2))
+        warm_out = sb.tile([P, 1], F32, name="warm_out")
+        nc.scalar.activation(warm_out[:], ident[:, 0:1], ACT.Exp)
+
+        q_raw = late.tile([P, PACK, Q], F32, name="q_raw", offset=0)
+        dq_raw = late.tile([P, PACK, Q], F32, name="dq_raw", offset=4 * V)
+        base_sb = [late.tile([P, V], F32, name=f"base{j}", offset=4 * V * (2 + j)) for j in range(TILES)]
+        store_words = late.tile([P, T], U32, name="store_words", offset=16 * V)
+        nc.sync.dma_start(store_words[:].bitcast(I32), summ_words[0].rearrange("p n t -> p (n t)").bitcast(I32))
+        nc.sync.dma_start(q_raw[:], query.rearrange("(p t) q -> p t q", t=PACK))
+        nc.sync.dma_start(dq_raw[:], dquery.rearrange("(p t) q -> p t q", t=PACK))
+        for j in range(TILES):
+            nc.sync.dma_start(base_sb[j][:], base[j * P : (j + 1) * P, :])
+
+        page_scales = sb.tile([P, U], U8, name="page_scales", align_bytes=64)
+        page_words = sb.tile([P, U], U32, name="page_words", align_bytes=64)
+        nc.vector.tensor_copy(page_scales[:], store_scales[:].indirect(page_list[:]))
+        nc.vector.tensor_copy(page_words[:], store_words[:].indirect(page_list[:]))
+
+        gain_bank = ps.tile([P, 2, P], F32, name="gain_bank")
+        for c in range(2):
+            nc.tensor.transpose(gain_bank[:, c, :], gain_pairs[:, c : c + 1].to_broadcast([P, P]), ident[:])
+        gain_row = sb.tile([P, I], F32, name="gain_row")
+        nc.scalar.activation(
+            gain_row[:].rearrange("p (s c) -> p s c", c=2), gain_bank[:].rearrange("p c s -> p s c"), ACT.Copy, scale=OUT_SCALE
+        )
+
+        def interleave(raw, j, name, on_vector):
+            grouped = sb.tile([P, P * PACK], BF16, name=name, align_bytes=64)
+            dst = grouped[:].rearrange("p (w t) -> p w t", t=PACK)
+            src = raw[:, :, j * P : (j + 1) * P].rearrange("p t w -> p w t")
+            if on_vector:
+                nc.vector.tensor_copy(dst, src)
+            else:
+                nc.scalar.copy(dst, src)
+            return grouped
+
+        def scores(grouped, name):
+            codes = sb.tile([P, P], U32, name=name + "_codes", align_bytes=64)
+            scales = sb.tile([P, P], U8, name=name + "_scales", align_bytes=64)
+            nc.vector.quantize_mx(out=codes[:].bitcast(FP8X4), scales=scales[:], in_=grouped[:])
+            bank = ps.tile([P, U], F32, name=name + "_bank")
+            nc.tensor.matmul_mx(
+                out=bank[:],
+                lhsT=codes[:].bitcast(FP8X4),
+                lhsT_scale=scales[:],
+                rhs=page_words[:].bitcast(FP8X4),
+                rhs_scale=page_scales[:],
+                start=True,
+                stop=True,
+            )
+            return bank
+
+        qg = [interleave(q_raw, j, f"qg{j}", j == 0) for j in range(TILES)]
+        a = [scores(qg[j], f"a{j}") for j in range(TILES)]
+        dqg = [interleave(dq_raw, j, f"dqg{j}", False) for j in range(TILES)]
+
+        neg_max = [sb.tile([P, 1], F32, name=f"neg_max{j}") for j in range(TILES)]
+        total = [sb.tile([P, 1], F32, name=f"total{j}") for j in range(TILES)]
+        inv = [sb.tile([P, 1], F32, name=f"inv{j}") for j in range(TILES)]
+        mean = [sb.tile([P, 1], F32, name=f"mean{j}") for j in range(TILES)]
+        p = [sb.tile([P, U], F32, name=f"p{j}") for j in range(TILES)]
+        w = [sb.tile([P, U], F32, name=f"w{j}") for j in range(TILES)]
+        wb = [sb.tile([P, U], F32, name=f"wb{j}") for j in range(TILES)]
+        dw = [sb.tile([P, U], F32, name=f"dw{j}") for j in range(TILES)]
+        picked_base = [sb.tile([P, I], F32, name=f"picked_base{j}") for j in range(TILES)]
+        picked_dw = [sb.tile([P, I], F32, name=f"picked_dw{j}") for j in range(TILES)]
+        result = [sb.tile([P, I], F32, name=f"result{j}") for j in range(TILES)]
+
+        for j in range(TILES):
+            nc.vector.tensor_reduce(neg_max[j][:], a[j][:], AXIS.X, ALU.max, negate=True)
+        b = [scores(dqg[j], f"b{j}") for j in range(TILES)]
+        for j in range(TILES):
+            nc.scalar.activation(p[j][:], a[j][:], ACT.Exp, bias=neg_max[j][:], scale=1.0, accum_out=total[j][:])
+            nc.vector.reciprocal(inv[j][:], total[j][:])
+            nc.scalar.activation(w[j][:], p[j][:], ACT.Copy, scale=inv[j][:])
+            nc.vector.tensor_copy(picked_base[j][:], base_sb[j][:].indirect(base_list[:]))
+            nc.vector.scalar_tensor_tensor(wb[j][:], b[j][:], 1.0, w[j][:], ALU.mult, ALU.mult, accum_out=mean[j][:])
+        for j in range(TILES):
+            nc.vector.scalar_tensor_tensor(dw[j][:], b[j][:], mean[j][:], w[j][:], ALU.subtract, ALU.mult)
+            nc.vector.tensor_tensor(picked_dw[j][:], dw[j][:].indirect(mass_list[:]), gain_row[:], ALU.mult)
+            nc.vector.scalar_tensor_tensor(result[j][:], picked_base[j][:], OUT_SCALE, picked_dw[j][:], ALU.mult, ALU.add)
+            nc.sync.dma_start(out[j * P : (j + 1) * P, :], result[j][:])

@@ -19,6 +19,7 @@ AXIS = mybir.AxisListType
 P = 128
 PACK = 4
 TILES = Q // P
+HALF = U // 2
 OUT_SCALE = 512.0
 
 
@@ -33,10 +34,11 @@ def tile_attend_masstangent_kernel(tc, query, dquery, summ_words, summ_scales, b
         mass_list = sb.tile([P, I // 16], U16, name="mass_list")
         base_list = sb.tile([P, I // 16], U16, name="base_list")
         store_scales = sb.tile([P, T], U8, name="store_scales", align_bytes=64)
-        gain_pairs = sb.tile([P, 2], F32, name="gain_pairs")
+        q_raw = sb.tile([P, PACK, Q], F32, name="q_raw")
 
-        nc.gpsimd.memset(store_scales[:].bitcast(I32), 0)
+        nc.vector.memset(store_scales[:].bitcast(I32), 0)
         nc.sync.dma_start(page_list[:], offs)
+        nc.sync.dma_start(q_raw[:], query.rearrange("(p t) q -> p t q", t=PACK))
         nc.sync.dma_start(base_list[:], offs3)
         nc.sync.dma_start(mass_list[:], offs2)
         for quad in range(4):
@@ -45,32 +47,86 @@ def tile_attend_masstangent_kernel(tc, query, dquery, summ_words, summ_scales, b
                 summ_scales[0, 4 * quad : 4 * quad + 4, :].bitcast(I32),
             )
 
-        zeros = late.tile([P, 4 * V + T], F32, name="zeros", offset=0)
+        zeros = late.tile([P, T + 3 * V + 8], F32, name="zeros", offset=0)
         ident = sb.tile([P, P], F32, name="ident")
         nc.gpsimd.memset(zeros[:, :P], 0.0)
         nc.gpsimd.affine_select(
             out=ident[:], in_=zeros[:, :P], compare_op=ALU.not_equal, fill=1.0, base=0, pattern=[[-1, P]], channel_multiplier=1
         )
-        nc.gpsimd.dma_start(gain_pairs[:], gain.rearrange("o (p c) -> (o p) c", c=2))
         warm_out = sb.tile([P, 1], F32, name="warm_out")
         nc.scalar.activation(warm_out[:], ident[:, 0:1], ACT.Exp)
 
-        q_raw = late.tile([P, PACK, Q], F32, name="q_raw", offset=0)
-        dq_raw = late.tile([P, PACK, Q], F32, name="dq_raw", offset=4 * V)
-        base_sb = [late.tile([P, V], F32, name=f"base{j}", offset=4 * V * (2 + j)) for j in range(TILES)]
-        store_words = late.tile([P, T], U32, name="store_words", offset=16 * V)
+        store_words = late.tile([P, T], U32, name="store_words", offset=0)
+        dq_raw = late.tile([P, PACK, Q], F32, name="dq_raw", offset=4 * T)
+        base_sb = [late.tile([P, V], F32, name=f"base{j}", offset=4 * T + 4 * V * (1 + j)) for j in range(TILES)]
+        gain_pairs = late.tile([P, 2], F32, name="gain_pairs", offset=4 * T + 12 * V)
         nc.sync.dma_start(store_words[:].bitcast(I32), summ_words[0].rearrange("p n t -> p (n t)").bitcast(I32))
-        nc.sync.dma_start(q_raw[:], query.rearrange("(p t) q -> p t q", t=PACK))
         nc.sync.dma_start(dq_raw[:], dquery.rearrange("(p t) q -> p t q", t=PACK))
         for j in range(TILES):
             nc.sync.dma_start(base_sb[j][:], base[j * P : (j + 1) * P, :])
+        nc.sync.dma_start(gain_pairs[:], gain.rearrange("o (p c) -> (o p) c", c=2))
+
+        def quantise(raw, name, tag):
+            grouped = sb.tile([P, Q * PACK], BF16, name=name + "_grouped", tag=tag, align_bytes=64)
+            nc.scalar.copy(grouped[:].rearrange("p (w t) -> p w t", t=PACK), raw[:].rearrange("p t w -> p w t"))
+            codes = sb.tile([P, Q], U32, name=name + "_codes", align_bytes=64)
+            scales = sb.tile([P, Q], U8, name=name + "_scales", align_bytes=64)
+            nc.vector.quantize_mx(out=codes[:].bitcast(FP8X4), scales=scales[:], in_=grouped[:])
+            return codes, scales
+
+        def product(bank, operand, j, pages):
+            codes, scales = operand
+            rows = slice(j * P, (j + 1) * P)
+            nc.tensor.matmul_mx(
+                out=bank[:, pages],
+                lhsT=codes[:, rows].bitcast(FP8X4),
+                lhsT_scale=scales[:, rows],
+                rhs=page_words[:, pages].bitcast(FP8X4),
+                rhs_scale=page_scales[:, pages],
+                start=True,
+                stop=True,
+            )
 
         page_scales = sb.tile([P, U], U8, name="page_scales", align_bytes=64)
-        page_words = sb.tile([P, U], U32, name="page_words", align_bytes=64)
         nc.vector.tensor_copy(page_scales[:], store_scales[:].indirect(page_list[:]))
-        nc.vector.tensor_copy(page_words[:], store_words[:].indirect(page_list[:]))
+        q_mx = quantise(q_raw, "q", "q_grouped_then_words")
+        page_words = sb.tile([P, U], U32, name="page_words", tag="q_grouped_then_words", align_bytes=64)
+        a = [ps.tile([P, U], F32, name=f"a{j}", tag=f"a{j}") for j in range(TILES)]
+        b = [ps.tile([P, U], F32, name=f"b{j}") for j in range(TILES)]
+        for h in range(2):
+            pages = slice(h * HALF, (h + 1) * HALF)
+            nc.vector.tensor_copy(page_words[:, pages], store_words[:].indirect(page_list[:, h * HALF // 16 : (h + 1) * HALF // 16]))
+            for j in range(TILES):
+                product(a[j], q_mx, j, pages)
 
-        gain_bank = ps.tile([P, 2, P], F32, name="gain_bank")
+        neg_max = [sb.tile([P, 1], F32, name=f"neg_max{j}") for j in range(TILES)]
+        total = [sb.tile([P, 1], F32, name=f"total{j}", tag=f"total_then_base{j}") for j in range(TILES)]
+        moment = [sb.tile([P, 1], F32, name=f"moment{j}") for j in range(TILES)]
+        inv = [sb.tile([P, 1], F32, name=f"inv{j}") for j in range(TILES)]
+        mean = [sb.tile([P, 1], F32, name=f"mean{j}") for j in range(TILES)]
+        p = [late.tile([P, U], F32, name=f"p{j}", offset=4 * T + 4 * U * j) for j in range(TILES)]
+        w = [sb.tile([P, U], F32, name=f"w{j}") for j in range(TILES)]
+        pb = [sb.tile([P, U], F32, name=f"pb{j}") for j in range(TILES)]
+        dw = [sb.tile([P, U], F32, name=f"dw{j}") for j in range(TILES)]
+        picked_dw = [sb.tile([P, I], F32, name=f"picked_dw{j}") for j in range(TILES)]
+        result = [sb.tile([P, I], F32, name=f"result{j}") for j in range(TILES)]
+
+        for j in range(TILES):
+            nc.vector.tensor_reduce(neg_max[j][:], a[j][:], AXIS.X, ALU.max, negate=True)
+        dq_mx = quantise(dq_raw, "dq", "dq_grouped_then_base")
+        for j in range(TILES):
+            product(b[j], dq_mx, j, slice(0, U))
+        for j in range(TILES):
+            nc.scalar.activation(p[j][:], a[j][:], ACT.Exp, bias=neg_max[j][:], scale=1.0, accum_out=total[j][:])
+            nc.vector.reciprocal(inv[j][:], total[j][:])
+        for j in range(TILES):
+            nc.scalar.activation(w[j][:], p[j][:], ACT.Copy, scale=inv[j][:])
+        for j in range(TILES):
+            nc.vector.scalar_tensor_tensor(pb[j][:], b[j][:], 1.0, p[j][:], ALU.mult, ALU.mult, accum_out=moment[j][:])
+            nc.gpsimd.tensor_tensor(mean[j][:], moment[j][:], inv[j][:], ALU.mult)
+        for j in range(TILES):
+            nc.vector.scalar_tensor_tensor(dw[j][:], b[j][:], mean[j][:], w[j][:], ALU.subtract, ALU.mult)
+        gain_bank = ps.tile([P, 2, P], F32, name="gain_bank", tag="a1")
         for c in range(2):
             nc.tensor.transpose(gain_bank[:, c, :], gain_pairs[:, c : c + 1].to_broadcast([P, P]), ident[:])
         gain_row = sb.tile([P, I], F32, name="gain_row")
@@ -78,59 +134,14 @@ def tile_attend_masstangent_kernel(tc, query, dquery, summ_words, summ_scales, b
             gain_row[:].rearrange("p (s c) -> p s c", c=2), gain_bank[:].rearrange("p c s -> p s c"), ACT.Copy, scale=OUT_SCALE
         )
 
-        def interleave(raw, j, name, on_vector):
-            grouped = sb.tile([P, P * PACK], BF16, name=name, align_bytes=64)
-            dst = grouped[:].rearrange("p (w t) -> p w t", t=PACK)
-            src = raw[:, :, j * P : (j + 1) * P].rearrange("p t w -> p w t")
-            if on_vector:
-                nc.vector.tensor_copy(dst, src)
-            else:
-                nc.scalar.copy(dst, src)
-            return grouped
-
-        def scores(grouped, name):
-            codes = sb.tile([P, P], U32, name=name + "_codes", align_bytes=64)
-            scales = sb.tile([P, P], U8, name=name + "_scales", align_bytes=64)
-            nc.vector.quantize_mx(out=codes[:].bitcast(FP8X4), scales=scales[:], in_=grouped[:])
-            bank = ps.tile([P, U], F32, name=name + "_bank")
-            nc.tensor.matmul_mx(
-                out=bank[:],
-                lhsT=codes[:].bitcast(FP8X4),
-                lhsT_scale=scales[:],
-                rhs=page_words[:].bitcast(FP8X4),
-                rhs_scale=page_scales[:],
-                start=True,
-                stop=True,
-            )
-            return bank
-
-        qg = [interleave(q_raw, j, f"qg{j}", j == 0) for j in range(TILES)]
-        a = [scores(qg[j], f"a{j}") for j in range(TILES)]
-        dqg = [interleave(dq_raw, j, f"dqg{j}", False) for j in range(TILES)]
-
-        neg_max = [sb.tile([P, 1], F32, name=f"neg_max{j}") for j in range(TILES)]
-        total = [sb.tile([P, 1], F32, name=f"total{j}") for j in range(TILES)]
-        inv = [sb.tile([P, 1], F32, name=f"inv{j}") for j in range(TILES)]
-        mean = [sb.tile([P, 1], F32, name=f"mean{j}") for j in range(TILES)]
-        p = [sb.tile([P, U], F32, name=f"p{j}") for j in range(TILES)]
-        w = [sb.tile([P, U], F32, name=f"w{j}") for j in range(TILES)]
-        wb = [sb.tile([P, U], F32, name=f"wb{j}") for j in range(TILES)]
-        dw = [sb.tile([P, U], F32, name=f"dw{j}") for j in range(TILES)]
-        picked_base = [sb.tile([P, I], F32, name=f"picked_base{j}") for j in range(TILES)]
-        picked_dw = [sb.tile([P, I], F32, name=f"picked_dw{j}") for j in range(TILES)]
-        result = [sb.tile([P, I], F32, name=f"result{j}") for j in range(TILES)]
-
+        picked_base = [
+            sb.tile([P, I], F32, name="picked_base0", tag="dq_grouped_then_base", align_bytes=64),
+            sb.tile([P, I], F32, name="picked_base1", tag="total_then_base1"),
+        ]
         for j in range(TILES):
-            nc.vector.tensor_reduce(neg_max[j][:], a[j][:], AXIS.X, ALU.max, negate=True)
-        b = [scores(dqg[j], f"b{j}") for j in range(TILES)]
-        for j in range(TILES):
-            nc.scalar.activation(p[j][:], a[j][:], ACT.Exp, bias=neg_max[j][:], scale=1.0, accum_out=total[j][:])
-            nc.vector.reciprocal(inv[j][:], total[j][:])
-            nc.scalar.activation(w[j][:], p[j][:], ACT.Copy, scale=inv[j][:])
             nc.vector.tensor_copy(picked_base[j][:], base_sb[j][:].indirect(base_list[:]))
-            nc.vector.scalar_tensor_tensor(wb[j][:], b[j][:], 1.0, w[j][:], ALU.mult, ALU.mult, accum_out=mean[j][:])
         for j in range(TILES):
-            nc.vector.scalar_tensor_tensor(dw[j][:], b[j][:], mean[j][:], w[j][:], ALU.subtract, ALU.mult)
             nc.vector.tensor_tensor(picked_dw[j][:], dw[j][:].indirect(mass_list[:]), gain_row[:], ALU.mult)
+        for j in range(TILES):
             nc.vector.scalar_tensor_tensor(result[j][:], picked_base[j][:], OUT_SCALE, picked_dw[j][:], ALU.mult, ALU.add)
             nc.sync.dma_start(out[j * P : (j + 1) * P, :], result[j][:])

@@ -41,11 +41,8 @@ def tile_attend_masstangent_kernel(tc, query, dquery, summ_words, summ_scales, b
         nc.sync.dma_start(q_raw[:], query.rearrange("(p t) q -> p t q", t=PACK))
         nc.sync.dma_start(base_list[:], offs3)
         nc.sync.dma_start(mass_list[:], offs2)
-        for quad in range(4):
-            nc.sync.dma_start(
-                store_scales[32 * quad : 32 * quad + 4, :].bitcast(I32),
-                summ_scales[0, 4 * quad : 4 * quad + 4, :].bitcast(I32),
-            )
+        for r in range(4):
+            nc.sync.dma_start(store_scales[r:P:32, :].bitcast(I32), summ_scales[0, r:16:4, :].bitcast(I32))
 
         zeros = late.tile([P, T + 3 * V + 8], F32, name="zeros", offset=0)
         ident = sb.tile([P, P], F32, name="ident")
@@ -66,9 +63,9 @@ def tile_attend_masstangent_kernel(tc, query, dquery, summ_words, summ_scales, b
             nc.sync.dma_start(base_sb[j][:], base[j * P : (j + 1) * P, :])
         nc.sync.dma_start(gain_pairs[:], gain.rearrange("o (p c) -> (o p) c", c=2))
 
-        def quantise(raw, name, tag):
+        def quantise(raw, name, tag, copy):
             grouped = sb.tile([P, Q * PACK], BF16, name=name + "_grouped", tag=tag, align_bytes=64)
-            nc.scalar.copy(grouped[:].rearrange("p (w t) -> p w t", t=PACK), raw[:].rearrange("p t w -> p w t"))
+            copy(grouped[:].rearrange("p (w t) -> p w t", t=PACK), raw[:].rearrange("p t w -> p w t"))
             codes = sb.tile([P, Q], U32, name=name + "_codes", align_bytes=64)
             scales = sb.tile([P, Q], U8, name=name + "_scales", align_bytes=64)
             nc.vector.quantize_mx(out=codes[:].bitcast(FP8X4), scales=scales[:], in_=grouped[:])
@@ -89,7 +86,7 @@ def tile_attend_masstangent_kernel(tc, query, dquery, summ_words, summ_scales, b
 
         page_scales = sb.tile([P, U], U8, name="page_scales", align_bytes=64)
         nc.vector.tensor_copy(page_scales[:], store_scales[:].indirect(page_list[:]))
-        q_mx = quantise(q_raw, "q", "q_grouped_then_words")
+        q_mx = quantise(q_raw, "q", "q_grouped_then_words", nc.vector.tensor_copy)
         page_words = sb.tile([P, U], U32, name="page_words", tag="q_grouped_then_words", align_bytes=64)
         a = [ps.tile([P, U], F32, name=f"a{j}", tag=f"a{j}") for j in range(TILES)]
         b = [ps.tile([P, U], F32, name=f"b{j}") for j in range(TILES)]
@@ -100,7 +97,7 @@ def tile_attend_masstangent_kernel(tc, query, dquery, summ_words, summ_scales, b
                 product(a[j], q_mx, j, pages)
 
         neg_max = [sb.tile([P, 1], F32, name=f"neg_max{j}") for j in range(TILES)]
-        total = [sb.tile([P, 1], F32, name=f"total{j}", tag=f"total_then_base{j}") for j in range(TILES)]
+        total = [sb.tile([P, 1], F32, name=f"total{j}", tag=f"total{j}") for j in range(TILES)]
         moment = [sb.tile([P, 1], F32, name=f"moment{j}") for j in range(TILES)]
         inv = [sb.tile([P, 1], F32, name=f"inv{j}") for j in range(TILES)]
         mean = [sb.tile([P, 1], F32, name=f"mean{j}") for j in range(TILES)]
@@ -113,7 +110,7 @@ def tile_attend_masstangent_kernel(tc, query, dquery, summ_words, summ_scales, b
 
         for j in range(TILES):
             nc.vector.tensor_reduce(neg_max[j][:], a[j][:], AXIS.X, ALU.max, negate=True)
-        dq_mx = quantise(dq_raw, "dq", "dq_grouped_then_base")
+        dq_mx = quantise(dq_raw, "dq", "dq_grouped", nc.scalar.copy)
         for j in range(TILES):
             product(b[j], dq_mx, j, slice(0, U))
         for j in range(TILES):
@@ -135,8 +132,8 @@ def tile_attend_masstangent_kernel(tc, query, dquery, summ_words, summ_scales, b
         )
 
         picked_base = [
-            sb.tile([P, I], F32, name="picked_base0", tag="dq_grouped_then_base", align_bytes=64),
-            sb.tile([P, I], F32, name="picked_base1", tag="total_then_base1"),
+            sb.tile([P, I], F32, name="picked_base0", tag="dq_grouped", align_bytes=64),
+            sb.tile([P, I], F32, name="picked_base1", tag="total1"),
         ]
         for j in range(TILES):
             nc.vector.tensor_copy(picked_base[j][:], base_sb[j][:].indirect(base_list[:]))

@@ -18,54 +18,67 @@ AXIS = mybir.AxisListType
 
 P = 128
 PACK = 4
+GROUP = 16
+QUADRANT = 32
+BLOCKS = D // 32
 TILES = Q // P
 HALF = U // 2
+LINE = 4
 OUT_SCALE = 512.0
+
+WORDS_AT = 0
+DQUERY_AT = WORDS_AT + 4 * T
+BASE_AT = DQUERY_AT + 4 * PACK * Q
+GAIN_AT = BASE_AT + 4 * TILES * V
+STAGED_BYTES = GAIN_AT + 32
 
 
 def tile_attend_masstangent_kernel(tc, query, dquery, summ_words, summ_scales, base, gain, offs, offs2, offs3, out):
     nc = tc.nc
     with ExitStack() as ctx:
         sb = ctx.enter_context(tc.tile_pool(name="sb", bufs=1))
-        late = ctx.enter_context(tc.tile_pool(name="late", bufs=1))
+        staged = ctx.enter_context(tc.tile_pool(name="staged", bufs=1))
         ps = ctx.enter_context(tc.psum_pool(name="ps", bufs=1))
 
-        page_list = sb.tile([P, U // 16], U16, name="page_list")
-        mass_list = sb.tile([P, I // 16], U16, name="mass_list")
-        base_list = sb.tile([P, I // 16], U16, name="base_list")
+        page_list = sb.tile([P, U // GROUP], U16, name="page_list")
+        mass_list = sb.tile([P, I // GROUP], U16, name="mass_list")
+        base_list = sb.tile([P, I // GROUP], U16, name="base_list")
         store_scales = sb.tile([P, T], U8, name="store_scales", align_bytes=64)
         q_raw = sb.tile([P, PACK, Q], F32, name="q_raw")
 
         nc.vector.memset(store_scales[:].bitcast(I32), 0)
         nc.sync.dma_start(page_list[:], offs)
-        nc.sync.dma_start(q_raw[:], query.rearrange("(p t) q -> p t q", t=PACK))
+        nc.sync.dma_start(q_raw[:], query.rearrange("(s t) q -> s t q", t=PACK))
         nc.sync.dma_start(base_list[:], offs3)
         nc.sync.dma_start(mass_list[:], offs2)
         for r in range(4):
-            nc.sync.dma_start(store_scales[r:P:32, :].bitcast(I32), summ_scales[0, r:16:4, :].bitcast(I32))
+            nc.sync.dma_start(
+                store_scales[r:P:QUADRANT, :].bitcast(I32), summ_scales[0, r:BLOCKS:4, :].bitcast(I32)
+            )
 
-        zeros = late.tile([P, T + 3 * V + 8], F32, name="zeros", offset=0)
+        zeros = staged.tile([P, STAGED_BYTES // 4], F32, name="zeros", offset=0)
         ident = sb.tile([P, P], F32, name="ident")
         nc.gpsimd.memset(zeros[:, :P], 0.0)
         nc.gpsimd.affine_select(
             out=ident[:], in_=zeros[:, :P], compare_op=ALU.not_equal, fill=1.0, base=0, pattern=[[-1, P]], channel_multiplier=1
         )
-        warm_out = sb.tile([P, 1], F32, name="warm_out")
-        nc.scalar.activation(warm_out[:], ident[:, 0:1], ACT.Exp)
 
-        store_words = late.tile([P, T], U32, name="store_words", offset=0)
-        dq_raw = late.tile([P, PACK, Q], F32, name="dq_raw", offset=4 * T)
-        base_sb = [late.tile([P, V], F32, name=f"base{j}", offset=4 * T + 4 * V * (1 + j)) for j in range(TILES)]
-        gain_pairs = late.tile([P, 2], F32, name="gain_pairs", offset=4 * T + 12 * V)
-        nc.sync.dma_start(store_words[:].bitcast(I32), summ_words[0].rearrange("p n t -> p (n t)").bitcast(I32))
-        nc.sync.dma_start(dq_raw[:], dquery.rearrange("(p t) q -> p t q", t=PACK))
+        store_words = staged.tile([P, T], U32, name="store_words", offset=WORDS_AT)
+        dq_raw = staged.tile([P, PACK, Q], F32, name="dq_raw", offset=DQUERY_AT)
+        base_sb = [staged.tile([P, V], F32, name=f"base{j}", offset=BASE_AT + 4 * V * j) for j in range(TILES)]
+        gain_pairs = staged.tile([P, 2], F32, name="gain_pairs", offset=GAIN_AT)
+        nc.sync.dma_start(store_words[:].bitcast(I32), summ_words[0].rearrange("s n t -> s (n t)").bitcast(I32))
+        nc.sync.dma_start(dq_raw[:], dquery.rearrange("(s t) q -> s t q", t=PACK))
         for j in range(TILES):
             nc.sync.dma_start(base_sb[j][:], base[j * P : (j + 1) * P, :])
-        nc.sync.dma_start(gain_pairs[:], gain.rearrange("o (p c) -> (o p) c", c=2))
+        nc.sync.dma_start(gain_pairs[:], gain.rearrange("o (s c) -> (o s) c", c=2))
 
         def quantise(raw, name, tag, copy):
             grouped = sb.tile([P, Q * PACK], BF16, name=name + "_grouped", tag=tag, align_bytes=64)
-            copy(grouped[:].rearrange("p (w t) -> p w t", t=PACK), raw[:].rearrange("p t w -> p w t"))
+            copy(
+                grouped[:].rearrange("s (c i t) -> s c t i", i=LINE, t=PACK),
+                raw[:].rearrange("s t (c i) -> s c t i", i=LINE),
+            )
             codes = sb.tile([P, Q], U32, name=name + "_codes", align_bytes=64)
             scales = sb.tile([P, Q], U8, name=name + "_scales", align_bytes=64)
             nc.vector.quantize_mx(out=codes[:].bitcast(FP8X4), scales=scales[:], in_=grouped[:])
@@ -86,22 +99,23 @@ def tile_attend_masstangent_kernel(tc, query, dquery, summ_words, summ_scales, b
 
         page_scales = sb.tile([P, U], U8, name="page_scales", align_bytes=64)
         nc.vector.tensor_copy(page_scales[:], store_scales[:].indirect(page_list[:]))
-        q_mx = quantise(q_raw, "q", "q_grouped_then_words", nc.vector.tensor_copy)
-        page_words = sb.tile([P, U], U32, name="page_words", tag="q_grouped_then_words", align_bytes=64)
+        q_mx = quantise(q_raw, "q", "q_grouped", nc.vector.tensor_copy)
+        page_words = sb.tile([P, U], U32, name="page_words", tag="q_grouped", align_bytes=64)
         a = [ps.tile([P, U], F32, name=f"a{j}", tag=f"a{j}") for j in range(TILES)]
         b = [ps.tile([P, U], F32, name=f"b{j}") for j in range(TILES)]
-        for h in range(2):
+        for h in range(U // HALF):
             pages = slice(h * HALF, (h + 1) * HALF)
-            nc.vector.tensor_copy(page_words[:, pages], store_words[:].indirect(page_list[:, h * HALF // 16 : (h + 1) * HALF // 16]))
+            entries = page_list[:, pages.start // GROUP : pages.stop // GROUP]
+            nc.vector.tensor_copy(page_words[:, pages], store_words[:].indirect(entries))
             for j in range(TILES):
                 product(a[j], q_mx, j, pages)
 
         neg_max = [sb.tile([P, 1], F32, name=f"neg_max{j}") for j in range(TILES)]
         total = [sb.tile([P, 1], F32, name=f"total{j}", tag=f"total{j}") for j in range(TILES)]
         moment = [sb.tile([P, 1], F32, name=f"moment{j}") for j in range(TILES)]
-        inv = [sb.tile([P, 1], F32, name=f"inv{j}") for j in range(TILES)]
+        inv_total = [sb.tile([P, 1], F32, name=f"inv_total{j}") for j in range(TILES)]
         mean = [sb.tile([P, 1], F32, name=f"mean{j}") for j in range(TILES)]
-        p = [late.tile([P, U], F32, name=f"p{j}", offset=4 * T + 4 * U * j) for j in range(TILES)]
+        p = [staged.tile([P, U], F32, name=f"p{j}", offset=DQUERY_AT + 4 * U * j) for j in range(TILES)]
         w = [sb.tile([P, U], F32, name=f"w{j}") for j in range(TILES)]
         pb = [sb.tile([P, U], F32, name=f"pb{j}") for j in range(TILES)]
         dw = [sb.tile([P, U], F32, name=f"dw{j}") for j in range(TILES)]
@@ -115,25 +129,26 @@ def tile_attend_masstangent_kernel(tc, query, dquery, summ_words, summ_scales, b
             product(b[j], dq_mx, j, slice(0, U))
         for j in range(TILES):
             nc.scalar.activation(p[j][:], a[j][:], ACT.Exp, bias=neg_max[j][:], scale=1.0, accum_out=total[j][:])
-            nc.vector.reciprocal(inv[j][:], total[j][:])
+            nc.vector.reciprocal(inv_total[j][:], total[j][:])
         for j in range(TILES):
-            nc.scalar.activation(w[j][:], p[j][:], ACT.Copy, scale=inv[j][:])
+            nc.scalar.activation(w[j][:], p[j][:], ACT.Copy, scale=inv_total[j][:])
         for j in range(TILES):
             nc.vector.scalar_tensor_tensor(pb[j][:], b[j][:], 1.0, p[j][:], ALU.mult, ALU.mult, accum_out=moment[j][:])
-            nc.gpsimd.tensor_tensor(mean[j][:], moment[j][:], inv[j][:], ALU.mult)
+            nc.scalar.activation(mean[j][:], moment[j][:], ACT.Copy, scale=inv_total[j][:])
         for j in range(TILES):
             nc.vector.scalar_tensor_tensor(dw[j][:], b[j][:], mean[j][:], w[j][:], ALU.subtract, ALU.mult)
-        gain_bank = ps.tile([P, 2, P], F32, name="gain_bank", tag="a1")
+
+        gain_bank = ps.tile([P, 2, P], F32, name="gain_bank", tag=f"a{TILES - 1}")
         for c in range(2):
             nc.tensor.transpose(gain_bank[:, c, :], gain_pairs[:, c : c + 1].to_broadcast([P, P]), ident[:])
         gain_row = sb.tile([P, I], F32, name="gain_row")
         nc.scalar.activation(
-            gain_row[:].rearrange("p (s c) -> p s c", c=2), gain_bank[:].rearrange("p c s -> p s c"), ACT.Copy, scale=OUT_SCALE
+            gain_row[:].rearrange("m (s c) -> m s c", c=2), gain_bank[:].rearrange("m c s -> m s c"), ACT.Copy, scale=OUT_SCALE
         )
 
         picked_base = [
             sb.tile([P, I], F32, name="picked_base0", tag="dq_grouped", align_bytes=64),
-            sb.tile([P, I], F32, name="picked_base1", tag="total1"),
+            sb.tile([P, I], F32, name="picked_base1", tag=f"total{TILES - 1}"),
         ]
         for j in range(TILES):
             nc.vector.tensor_copy(picked_base[j][:], base_sb[j][:].indirect(base_list[:]))

from contextlib import ExitStack

import concourse.mybir as mybir

D, U, T, I, V, Q = 512, 512, 2048, 256, 1024, 256
FLOPS = 2 * 2 * D * Q * U

F32 = mybir.dt.float32
BF16 = mybir.dt.bfloat16
I32 = mybir.dt.int32
U32 = mybir.dt.uint32
U16 = mybir.dt.uint16
U8 = mybir.dt.uint8
FP8X4 = mybir.dt.float8_e4m3fn_x4
ALU = mybir.AluOpType
ACT = mybir.ActivationFunctionType
AXIS = mybir.AxisListType

P = 128
PACK = 4
GROUP = 16
QUADRANT = 32
BLOCKS = D // 32
TILES = Q // P
HALF = U // 2
LINE = 4
OUT_SCALE = 512.0

WORDS_AT = 0
DQUERY_AT = WORDS_AT + 4 * T
BASE_AT = DQUERY_AT + 4 * PACK * Q
GAIN_AT = BASE_AT + 4 * TILES * V
STAGED_BYTES = GAIN_AT + 32


def tile_attend_masstangent_kernel(tc, query, dquery, summ_words, summ_scales, base, gain, offs, offs2, offs3, out):
    nc = tc.nc
    with ExitStack() as ctx:
        sb = ctx.enter_context(tc.tile_pool(name="sb", bufs=1))
        staged = ctx.enter_context(tc.tile_pool(name="staged", bufs=1))
        ps = ctx.enter_context(tc.psum_pool(name="ps", bufs=1))

        page_list = sb.tile([P, U // GROUP], U16, name="page_list")
        mass_list = sb.tile([P, I // GROUP], U16, name="mass_list")
        base_list = sb.tile([P, I // GROUP], U16, name="base_list")
        store_scales = sb.tile([P, T], U8, name="store_scales", align_bytes=64)
        q_raw = sb.tile([P, PACK, Q], F32, name="q_raw")

        nc.vector.memset(store_scales[:].bitcast(I32), 0)
        nc.sync.dma_start(page_list[:], offs)
        nc.sync.dma_start(q_raw[:], query.rearrange("(s t) q -> s t q", t=PACK))
        nc.sync.dma_start(base_list[:], offs3)
        nc.sync.dma_start(mass_list[:], offs2)
        for r in range(4):
            nc.sync.dma_start(
                store_scales[r:P:QUADRANT, :].bitcast(I32), summ_scales[0, r:BLOCKS:4, :].bitcast(I32)
            )

        zeros = staged.tile([P, STAGED_BYTES // 4], F32, name="zeros", offset=0)
        ident = sb.tile([P, P], F32, name="ident")
        nc.gpsimd.memset(zeros[:, :P], 0.0)
        nc.gpsimd.affine_select(
            out=ident[:], in_=zeros[:, :P], compare_op=ALU.not_equal, fill=1.0, base=0, pattern=[[-1, P]], channel_multiplier=1
        )

        store_words = staged.tile([P, T], U32, name="store_words", offset=WORDS_AT)
        dq_raw = staged.tile([P, PACK, Q], F32, name="dq_raw", offset=DQUERY_AT)
        base_sb = [staged.tile([P, V], F32, name=f"base{j}", offset=BASE_AT + 4 * V * j) for j in range(TILES)]
        gain_pairs = staged.tile([P, 2], F32, name="gain_pairs", offset=GAIN_AT)
        nc.sync.dma_start(store_words[:].bitcast(I32), summ_words[0].rearrange("s n t -> s (n t)").bitcast(I32))
        nc.sync.dma_start(dq_raw[:], dquery.rearrange("(s t) q -> s t q", t=PACK))
        for j in range(TILES):
            nc.sync.dma_start(base_sb[j][:], base[j * P : (j + 1) * P, :])
        nc.sync.dma_start(gain_pairs[:], gain.rearrange("o (s c) -> (o s) c", c=2))

        def quantise(raw, name, tag, copy):
            grouped = sb.tile([P, Q * PACK], BF16, name=name + "_grouped", tag=tag, align_bytes=64)
            copy(
                grouped[:].rearrange("s (c i t) -> s c t i", i=LINE, t=PACK),
                raw[:].rearrange("s t (c i) -> s c t i", i=LINE),
            )
            codes = sb.tile([P, Q], U32, name=name + "_codes", align_bytes=64)
            scales = sb.tile([P, Q], U8, name=name + "_scales", align_bytes=64)
            nc.vector.quantize_mx(out=codes[:].bitcast(FP8X4), scales=scales[:], in_=grouped[:])
            return codes, scales

        def product(bank, operand, j, pages):
            codes, scales = operand
            rows = slice(j * P, (j + 1) * P)
            nc.tensor.matmul_mx(
                out=bank[:, pages],
                lhsT=codes[:, rows].bitcast(FP8X4),
                lhsT_scale=scales[:, rows],
                rhs=page_words[:, pages].bitcast(FP8X4),
                rhs_scale=page_scales[:, pages],
                start=True,
                stop=True,
            )

        page_scales = sb.tile([P, U], U8, name="page_scales", align_bytes=64)
        nc.vector.tensor_copy(page_scales[:], store_scales[:].indirect(page_list[:]))
        q_mx = quantise(q_raw, "q", "q_grouped", nc.vector.tensor_copy)
        page_words = sb.tile([P, U], U32, name="page_words", tag="q_grouped", align_bytes=64)
        a = [ps.tile([P, U], F32, name=f"a{j}", tag=f"a{j}") for j in range(TILES)]
        b = [ps.tile([P, U], F32, name=f"b{j}") for j in range(TILES)]
        for h in range(U // HALF):
            pages = slice(h * HALF, (h + 1) * HALF)
            entries = page_list[:, pages.start // GROUP : pages.stop // GROUP]
            nc.vector.tensor_copy(page_words[:, pages], store_words[:].indirect(entries))
            for j in range(TILES):
                product(a[j], q_mx, j, pages)

        neg_max = [sb.tile([P, 1], F32, name=f"neg_max{j}") for j in range(TILES)]
        total = [sb.tile([P, 1], F32, name=f"total{j}", tag=f"total{j}") for j in range(TILES)]
        moment = [sb.tile([P, 1], F32, name=f"moment{j}") for j in range(TILES)]
        inv_total = [sb.tile([P, 1], F32, name=f"inv_total{j}") for j in range(TILES)]
        mean = [sb.tile([P, 1], F32, name=f"mean{j}") for j in range(TILES)]
        p = [staged.tile([P, U], F32, name=f"p{j}", offset=DQUERY_AT + 4 * U * j) for j in range(TILES)]
        w = [sb.tile([P, U], F32, name=f"w{j}") for j in range(TILES)]
        pb = [sb.tile([P, U], F32, name=f"pb{j}") for j in range(TILES)]
        dw = [sb.tile([P, U], F32, name=f"dw{j}") for j in range(TILES)]
        picked_dw = [sb.tile([P, I], F32, name=f"picked_dw{j}") for j in range(TILES)]
        result = [sb.tile([P, I], F32, name=f"result{j}") for j in range(TILES)]

        for j in range(TILES):
            nc.vector.tensor_reduce(neg_max[j][:], a[j][:], AXIS.X, ALU.max, negate=True)
        dq_mx = quantise(dq_raw, "dq", "dq_grouped", nc.scalar.copy)
        for j in range(TILES):
            product(b[j], dq_mx, j, slice(0, U))
        for j in range(TILES):
            nc.scalar.activation(p[j][:], a[j][:], ACT.Exp, bias=neg_max[j][:], scale=1.0, accum_out=total[j][:])
            nc.vector.reciprocal(inv_total[j][:], total[j][:])
        for j in range(TILES):
            nc.scalar.activation(w[j][:], p[j][:], ACT.Copy, scale=inv_total[j][:])
        for j in range(TILES):
            nc.vector.scalar_tensor_tensor(pb[j][:], b[j][:], 1.0, p[j][:], ALU.mult, ALU.mult, accum_out=moment[j][:])
            nc.scalar.activation(mean[j][:], moment[j][:], ACT.Copy, scale=inv_total[j][:])
        for j in range(TILES):
            nc.vector.scalar_tensor_tensor(dw[j][:], b[j][:], mean[j][:], w[j][:], ALU.subtract, ALU.mult)

        gain_bank = ps.tile([P, 2, P], F32, name="gain_bank", tag=f"a{TILES - 1}")
        for c in range(2):
            nc.tensor.transpose(gain_bank[:, c, :], gain_pairs[:, c : c + 1].to_broadcast([P, P]), ident[:])
        gain_row = sb.tile([P, I], F32, name="gain_row")
        nc.scalar.activation(
            gain_row[:].rearrange("m (s c) -> m s c", c=2), gain_bank[:].rearrange("m c s -> m s c"), ACT.Copy, scale=OUT_SCALE
        )

        picked_base = [
            sb.tile([P, I], F32, name="picked_base0", tag="dq_grouped", align_bytes=64),
            sb.tile([P, I], F32, name="picked_base1", tag=f"total{TILES - 1}"),
        ]
        for j in range(TILES):
            nc.vector.tensor_copy(picked_base[j][:], base_sb[j][:].indirect(base_list[:]))
        for j in range(TILES):
            nc.vector.tensor_tensor(picked_dw[j][:], dw[j][:].indirect(mass_list[:]), gain_row[:], ALU.mult)
        for j in range(TILES):
            nc.vector.scalar_tensor_tensor(result[j][:], picked_base[j][:], OUT_SCALE, picked_dw[j][:], ALU.mult, ALU.add)
            nc.sync.dma_start(out[j * P : (j + 1) * P, :], result[j][:])
